import numpy as np
import ml_dtypes


def mxq(x, axis, fmt="e4m3"):
    dtype, down = {"e4m3": (ml_dtypes.float8_e4m3fn, 7), "e5m2": (ml_dtypes.float8_e5m2, 14)}[fmt]
    v = np.moveaxis(np.asarray(x, np.float32).astype(ml_dtypes.bfloat16).astype(np.float64), axis, -1)
    blocks = v.reshape(v.shape[:-1] + (-1, 32))
    amax = np.abs(blocks).max(-1, keepdims=True)
    byte = np.maximum(np.where(amax > 0, np.frexp(amax)[1] - 1 + 127, 0) - down, 1)
    scale = np.exp2(byte - 127.0)
    codes = (blocks / scale).astype(np.float32).astype(dtype).astype(np.float64)
    return np.moveaxis((codes * scale).reshape(v.shape), -1, axis)


WIDE = False


def mx_kscale(k):
    if not WIDE:
        return np.ones(k)
    levels = np.array([10, -10, 5, -5, 0])
    if k % 512:
        return np.exp2(np.random.permutation(np.resize(levels, k // 32))).repeat(32)
    a = np.empty((k // 512, 16))
    for p in range(k // 512):
        a[p, :8] = np.random.permutation(np.resize(levels, 8))
        for g in range(8):
            far = levels[np.abs(levels - a[p, g]) >= 10]
            a[p, g + 8] = far[np.random.randint(len(far))]
    return np.exp2(a.ravel()).repeat(32)


def f64(x):
    return np.asarray(x).astype(np.float64)


def striped(idx):
    return np.tile(idx.reshape(-1, 16).T, (8, 1)).astype(np.uint16)


def unstriped(offs):
    return offs[:16].T.reshape(-1).astype(np.int64)


def striped8(idx):
    return np.concatenate([x.reshape(-1, 16).T for x in idx]).astype(np.uint16)


def runs(offs, k):
    lists = np.stack([offs[16 * r : 16 * r + 16].T.reshape(-1) for r in range(8)]).astype(np.int64)
    return lists[np.arange(k) % 512 // 64]


def pack_weight(w):
    k, n = w.shape
    w = f64(np.asarray(w, np.float32).astype(ml_dtypes.bfloat16)).reshape(k // 32, 32, n)
    amax = np.abs(w).max(1)
    byte = np.clip(np.where(amax > 0, np.frexp(amax)[1] - 1 + 127 - 7, 1), 1, 254)
    scaled = (w * np.exp2(127.0 - byte)[:, None, :]).reshape(k, n).astype(np.float32)
    words = np.ascontiguousarray(scaled.reshape(k // 512, 128, 4, n).transpose(0, 1, 3, 2)).astype(ml_dtypes.float8_e4m3fn).view(np.uint8)
    return words, np.ascontiguousarray(byte.astype(np.uint8).reshape(k // 512, 16, n))


def unpack_weight(words, scales):
    g, p, n, _ = words.shape
    vals = np.ascontiguousarray(words).view(ml_dtypes.float8_e4m3fn).astype(np.float64) * np.repeat(np.exp2(scales.astype(np.float64) - 127.0), 8, axis=1)[..., None]
    return vals.transpose(0, 1, 3, 2).reshape(g * 512, n)


def relu(v):
    return np.maximum(v, 0.0)


K, T, S, N, H = 512, 2048, 512, 512, 512


def setup_inputs():
    n = np.random.standard_normal
    s = mx_kscale(K)[:, None]
    u = mx_kscale(H)
    packed_xT = pack_weight(n((K, T)) * s)
    return {
        "x_words": packed_xT[0],
        "x_scales": packed_xT[1],
        "w1": (n((K, H)) / np.sqrt(K) / s).astype(np.float32),
        "gn": (np.random.uniform(0.5, 1.5, (H, 1)) * u[:, None]).astype(np.float32),
        "w2": (n((H, N)) / np.sqrt(H) / u[:, None]).astype(np.float32),
        "offs": striped(np.random.permutation(T)[:S]),
        "n1": striped8(np.stack([np.random.permutation(S) for _ in range(8)])),
        "n2": striped8(np.stack([np.random.permutation(S) for _ in range(8)])),
        "n3": striped8(np.stack([np.random.permutation(S) for _ in range(8)])),
    }


def reference(x_words, x_scales, w1, gn, w2, offs, n1, n2, n3):
    xq = unpack_weight(x_words, x_scales)[:, unstriped(offs)]
    y = mxq(f64(w1), 0, "e4m3").T @ xq
    ex = np.exp(-1.0 * y)
    z = f64(gn) * (-1.0 * (np.log(ex + ex[np.arange(H)[:, None], runs(n1, H)])))
    h = mxq(f64(w2), 0, "e4m3").T @ mxq(z, 0, "e4m3")
    return relu(np.maximum(h[np.arange(N)[:, None], runs(n2, N)], h[np.arange(N)[:, None], runs(n3, N)]) - h + 0.5)

@@ -1,0 +1,248 @@
+from contextlib import ExitStack
+
+import concourse.mybir as mybir
+
+K, T, S, H, N = 512, 2048, 512, 512, 512
+FLOPS = 2 * K * H * S + 2 * H * N * S
+
+F32 = mybir.dt.float32
+BF16 = mybir.dt.bfloat16
+I32 = mybir.dt.int32
+U32 = mybir.dt.uint32
+U16 = mybir.dt.uint16
+U8 = mybir.dt.uint8
+FP8X4 = mybir.dt.float8_e4m3fn_x4
+ACT = mybir.ActivationFunctionType
+ALU = mybir.AluOpType
+
+P = 128
+PACK = 4
+HALF = S // 2
+QUARTER = S // 4
+LIST_COLS = S // 16
+
+
+def tile_picked_sminhinge_none_p_kernel(
+    tc, x_words, x_scales, w1, gn, w2, offs, n1, n2, n3, out
+):
+    nc = tc.nc
+    with ExitStack() as ctx:
+        keep = ctx.enter_context(tc.tile_pool(name="keep", bufs=1))
+        psum = ctx.enter_context(tc.psum_pool(name="psum", bufs=1))
+
+        def cols(part, width):
+            return slice(part * width, (part + 1) * width)
+
+        def load_list(name, source):
+            tile = keep.tile([P, LIST_COLS], U16, name=name)
+            nc.sync.dma_start(tile[:], source)
+            return tile
+
+        def load_weight_half(name, w, half):
+            raw = keep.tile([P, PACK, HALF], F32, name="%s_raw%d" % (name, half))
+            nc.sync.dma_start(raw[:], w.rearrange("(p j) c -> p j c", j=PACK)[:, :, cols(half, HALF)])
+            return raw
+
+        def deal_views(grouped, raw, half):
+            dst = grouped[:].rearrange("p (t m j) -> p m j t", t=PACK, j=PACK)[:, cols(half, P // 2), :, :]
+            src = raw[:].rearrange("p j (m t) -> p m j t", t=PACK)
+            return dst, src
+
+        def bank(index):
+            return psum.tile([P, S], F32, name="bank%d" % index, tag="bank%d" % index)
+
+        x_scale_table = keep.tile([P, T], U8, name="x_scale_table")
+        nc.vector.memset(x_scale_table[:].bitcast(I32), 0)
+        w1_raw = [load_weight_half("w1", w1, 0)]
+        for q in range(4):
+            nc.sync.dma_start(
+                x_scale_table[32 * q : 32 * q + 4, :].bitcast(I32), x_scales[0, 4 * q : 4 * q + 4, :].bitcast(I32)
+            )
+        w1_raw.append(load_weight_half("w1", w1, 1))
+        offs_sb = load_list("offs_sb", offs)
+        x_word_table = keep.tile([P, T], I32, name="x_word_table")
+        nc.sync.dma_start(x_word_table[:], x_words[0].rearrange("p n t -> p (n t)").bitcast(I32))
+        n1_sb = load_list("n1_sb", n1)
+        w2_raw = keep.tile([P, PACK, N], F32, name="w2_raw")
+        nc.sync.dma_start(w2_raw[:], w2.rearrange("(p j) c -> p j c", j=PACK))
+        gain = keep.tile([P, PACK], F32, name="gain")
+        nc.sync.dma_start(gain[:], gn.rearrange("(p t) one -> p (t one)", t=PACK))
+        n2_sb = load_list("n2_sb", n2)
+        n3_sb = load_list("n3_sb", n3)
+
+        w1_grouped = keep.tile([P, PACK * H], BF16, name="w1_grouped", align_bytes=64)
+        dst, src = deal_views(w1_grouped, w1_raw[0], 0)
+        nc.scalar.activation(dst, src, ACT.Copy)
+        dst, src = deal_views(w1_grouped, w1_raw[1], 1)
+        nc.vector.tensor_copy(dst, src)
+        x_scale_picked = keep.tile([P, S], U8, name="x_scale_picked", align_bytes=64)
+        nc.vector.tensor_copy(x_scale_picked[:], x_scale_table[:].indirect(offs_sb[:]))
+        w1_codes = keep.tile([P, H], U32, name="w1_codes", align_bytes=64)
+        w1_scales = keep.tile([P, H], U8, name="w1_scales", align_bytes=64)
+        nc.vector.quantize_mx(out=w1_codes[:].bitcast(FP8X4), scales=w1_scales[:], in_=w1_grouped[:])
+
+        x_picked = []
+        for half in range(2):
+            words = keep.tile([P, HALF], U32, name="x_picked%d" % half, align_bytes=64)
+            nc.vector.tensor_copy(
+                words[:], x_word_table[:].bitcast(U32).indirect(offs_sb[:, cols(half, LIST_COLS // 2)])
+            )
+            x_picked.append(words)
+
+        ex_window = [keep.tile([P, S], F32, name="ex_window%d" % t) for t in range(PACK)]
+        ex_plain = [keep.tile([P, S], F32, name="ex_plain%d" % t) for t in range(PACK)]
+        sums = [keep.tile([P, PACK, HALF], F32, name="sums%d" % half) for half in range(2)]
+
+        def first_product(target, t, half):
+            nc.tensor.matmul_mx(
+                out=target[:, cols(half, HALF)],
+                lhsT=w1_codes[:, cols(t, P)].bitcast(FP8X4),
+                lhsT_scale=w1_scales[:, cols(t, P)],
+                rhs=x_picked[half][:].bitcast(FP8X4),
+                rhs_scale=x_scale_picked[:, cols(half, HALF)],
+                start=True,
+                stop=True,
+            )
+
+        def exponential(target, source, columns):
+            nc.scalar.activation(target[:, columns], source[:, columns], ACT.Exp, scale=-1.0)
+
+        def pair_sums(t, half):
+            nc.vector.tensor_tensor(
+                sums[half][:, t, :],
+                ex_window[t][:].indirect(n1_sb[:, cols(half, LIST_COLS // 2)]),
+                ex_plain[t][:, cols(half, HALF)],
+                ALU.add,
+            )
+
+        def w2_views(grouped, t):
+            dst = grouped[:].rearrange("p (b c i j) -> p b c j i", b=16, c=2, i=4)
+            src = w2_raw[:].rearrange("p j (b t c i) -> p t b c j i", b=16, t=PACK, c=2)[:, t]
+            return dst, src
+
+        def w2_quantize(grouped, t):
+            codes = keep.tile([P, P], U32, name="w2_codes%d" % t, tag="w2_slot%d" % t, align_bytes=64)
+            scales = keep.tile([P, P], U8, name="w2_scales%d" % t, align_bytes=64)
+            nc.vector.quantize_mx(out=codes[:].bitcast(FP8X4), scales=scales[:], in_=grouped[:])
+            return codes, scales
+
+        whole = slice(0, S)
+        for half in range(2):
+            y_half = bank(half)
+            first_product(y_half, 0, half)
+            exponential(ex_window[0], y_half, cols(half, HALF))
+            exponential(ex_plain[0], y_half, cols(half, HALF))
+        y_bank = {}
+        for t in (3, 1, 2):
+            y_bank[t] = bank(1 + t)
+            for half in range(2):
+                first_product(y_bank[t], t, half)
+        exponential(ex_window[3], y_bank[3], whole)
+        nc.sync.dma_start(ex_plain[3][:], ex_window[3][:])
+        for half in range(2):
+            pair_sums(0, half)
+        w2_first = keep.tile([P, PACK * P], BF16, name="w2_grouped0", align_bytes=64)
+        nc.vector.tensor_copy(*w2_views(w2_first, 0))
+        for t in (1, 2):
+            exponential(ex_window[t], y_bank[t], whole)
+            exponential(ex_plain[t], y_bank[t], whole)
+        pair_sums(1, 0)
+        w2_quantized = [w2_quantize(w2_first, 0)]
+        pair_sums(1, 1)
+        for half in range(2):
+            for t in (2, 3):
+                pair_sums(t, half)
+
+        z_codes = keep.tile([P, S], U32, name="z_codes", align_bytes=64)
+        z_scales = keep.tile([P, S], U8, name="z_scales", align_bytes=64)
+        z_rounded = []
+        for quarter in range(4):
+            logs = keep.tile([P, QUARTER, PACK], F32, name="logs%d" % quarter)
+            nc.scalar.activation(
+                logs[:].rearrange("p (c i) t -> p c t i", i=4),
+                sums[quarter // 2][:, :, cols(quarter % 2, QUARTER)].rearrange("p t (c i) -> p c t i", i=4),
+                ACT.Ln,
+            )
+            rounded = keep.tile([P, QUARTER * PACK], BF16, name="z_rounded%d" % quarter, tag="z_slot%d" % quarter, align_bytes=64)
+            nc.vector.scalar_tensor_tensor(
+                rounded[:].rearrange("p (n t) -> p n t", t=PACK),
+                logs[:],
+                -1.0,
+                gain[:].unsqueeze(1).to_broadcast([P, QUARTER, PACK]),
+                ALU.mult,
+                ALU.mult,
+            )
+            z_rounded.append(rounded)
+            if quarter > 0:
+                nc.vector.quantize_mx(
+                    out=z_codes[:, cols(quarter - 1, QUARTER)].bitcast(FP8X4),
+                    scales=z_scales[:, cols(quarter - 1, QUARTER)],
+                    in_=z_rounded[quarter - 1][:],
+                )
+        nc.vector.quantize_mx(
+            out=z_codes[:, cols(3, QUARTER)].bitcast(FP8X4), scales=z_scales[:, cols(3, QUARTER)], in_=z_rounded[3][:]
+        )
+
+        h_window = [keep.tile([P, S], F32, name="h_window%d" % t) for t in range(PACK)]
+        h_less = [keep.tile([P, S], F32, name="h_less%d" % t) for t in range(PACK)]
+
+        def second_product(target, t, columns):
+            nc.tensor.matmul_mx(
+                out=target[:, columns],
+                lhsT=w2_quantized[t][0][:].bitcast(FP8X4),
+                lhsT_scale=w2_quantized[t][1][:],
+                rhs=z_codes[:, columns].bitcast(FP8X4),
+                rhs_scale=z_scales[:, columns],
+                start=True,
+                stop=True,
+            )
+
+        def leave_bank(source, t, columns):
+            nc.scalar.activation(h_window[t][:, columns], source[:, columns], ACT.Copy)
+            nc.scalar.activation(h_less[t][:, columns], source[:, columns], ACT.Copy, bias=-0.5)
+
+        early, late = bank(5), bank(6)
+        for quarter in range(3):
+            second_product(early, 0, cols(quarter, QUARTER))
+        leave_bank(early, 0, slice(0, 3 * QUARTER))
+        second_product(late, 0, cols(3, QUARTER))
+        leave_bank(late, 0, cols(3, QUARTER))
+        for t in range(1, PACK):
+            if t == 1:
+                grouped = keep.tile([P, PACK * P], BF16, name="w2_grouped1", tag="z_slot3", align_bytes=64)
+                nc.vector.tensor_copy(*w2_views(grouped, t))
+            else:
+                grouped = keep.tile(
+                    [P, PACK * P], BF16, name="w2_grouped%d" % t, tag="w2_slot%d" % (t - 2), align_bytes=64
+                )
+                nc.scalar.copy(*w2_views(grouped, t))
+            w2_quantized.append(w2_quantize(grouped, t))
+            h_bank = bank(t - 1)
+            second_product(h_bank, t, whole)
+            leave_bank(h_bank, t, whole)
+
+        out_rows = out.rearrange("(b t s) n -> t b s n", b=16, t=PACK)
+        steps = [(t, half) for t in range(PACK) for half in range(2)]
+        margins = {}
+
+        def finish(t, half):
+            result = keep.tile([P, HALF], F32, name="result%d_%d" % (t, half))
+            a, b = margins[t, half]
+            nc.vector.scalar_tensor_tensor(result[:], a[:], 0.0, b[:], ALU.max, ALU.max)
+            nc.sync.dma_start(out_rows[t][:, :, cols(half, HALF)], result[:])
+
+        for index, (t, half) in enumerate(steps):
+            pair = []
+            for name, places in (("a", n2_sb), ("b", n3_sb)):
+                margin = keep.tile([P, HALF], F32, name="margin_%s%d_%d" % (name, t, half))
+                nc.vector.tensor_tensor(
+                    margin[:],
+                    h_window[t][:].indirect(places[:, cols(half, LIST_COLS // 2)]),
+                    h_less[t][:, cols(half, HALF)],
+                    ALU.subtract,
+                )
+                pair.append(margin)
+                if name == "a" and index > 0:
+                    finish(*steps[index - 1])
+            margins[t, half] = pair
+        finish(*steps[-1])

@@ -1,6 +1,7 @@
 from contextlib import ExitStack
 
 import concourse.mybir as mybir
+from concourse.masks import make_identity
 
 K, T, S, H, N = 512, 2048, 512, 512, 512
 FLOPS = 2 * K * H * S + 2 * H * N * S
@@ -20,6 +21,7 @@ PACK = 4
 HALF = S // 2
 QUARTER = S // 4
 LIST_COLS = S // 16
+TURNED = 1
 
 
 def tile_picked_sminhinge_none_p_kernel(
@@ -53,13 +55,11 @@ def tile_picked_sminhinge_none_p_kernel(
 
         x_scale_table = keep.tile([P, T], U8, name="x_scale_table")
         nc.vector.memset(x_scale_table[:].bitcast(I32), 0)
-        w1_raw = [load_weight_half("w1", w1, 0)]
-        for q in range(4):
-            nc.sync.dma_start(
-                x_scale_table[32 * q : 32 * q + 4, :].bitcast(I32), x_scales[0, 4 * q : 4 * q + 4, :].bitcast(I32)
-            )
-        w1_raw.append(load_weight_half("w1", w1, 1))
         offs_sb = load_list("offs_sb", offs)
+        w1_raw = [load_weight_half("w1", w1, 0)]
+        for r in range(4):
+            nc.sync.dma_start(x_scale_table[r:P:32, :].bitcast(I32), x_scales[0, r:16:4, :].bitcast(I32))
+        w1_raw.append(load_weight_half("w1", w1, 1))
         x_word_table = keep.tile([P, T], I32, name="x_word_table")
         nc.sync.dma_start(x_word_table[:], x_words[0].rearrange("p n t -> p (n t)").bitcast(I32))
         n1_sb = load_list("n1_sb", n1)
@@ -69,6 +69,11 @@ def tile_picked_sminhinge_none_p_kernel(
         nc.sync.dma_start(gain[:], gn.rearrange("(p t) one -> p (t one)", t=PACK))
         n2_sb = load_list("n2_sb", n2)
         n3_sb = load_list("n3_sb", n3)
+
+        identity = keep.tile([P, P], F32, name="identity")
+        make_identity(nc, identity[:])
+        one_half = keep.tile([P, 1], F32, name="one_half")
+        nc.gpsimd.memset(one_half[:], 0.5)
 
         w1_grouped = keep.tile([P, PACK * H], BF16, name="w1_grouped", align_bytes=64)
         dst, src = deal_views(w1_grouped, w1_raw[0], 0)
@@ -89,8 +94,10 @@ def tile_picked_sminhinge_none_p_kernel(
             )
             x_picked.append(words)
 
-        ex_window = [keep.tile([P, S], F32, name="ex_window%d" % t) for t in range(PACK)]
-        ex_plain = [keep.tile([P, S], F32, name="ex_plain%d" % t) for t in range(PACK)]
+        first_window = keep.tile([P, S], F32, name="first_window")
+        wide = [keep.tile([P, 2 * S], F32, name="wide%d" % t) for t in range(PACK)]
+        ex_window = [first_window, wide[1], wide[2], wide[3]]
+        ex_plain = [wide[t ^ 1][:, S : 2 * S] for t in range(PACK)]
         sums = [keep.tile([P, PACK, HALF], F32, name="sums%d" % half) for half in range(2)]
 
         def first_product(target, t, half):
@@ -107,11 +114,15 @@ def tile_picked_sminhinge_none_p_kernel(
         def exponential(target, source, columns):
             nc.scalar.activation(target[:, columns], source[:, columns], ACT.Exp, scale=-1.0)
 
+        def entries(places, columns):
+            return places[:, columns.start // 16 : columns.stop // 16]
+
         def pair_sums(t, half):
+            columns = cols(half, HALF)
             nc.vector.tensor_tensor(
                 sums[half][:, t, :],
-                ex_window[t][:].indirect(n1_sb[:, cols(half, LIST_COLS // 2)]),
-                ex_plain[t][:, cols(half, HALF)],
+                ex_window[t][:].indirect(entries(n1_sb, columns)),
+                ex_plain[t][:, columns],
                 ALU.add,
             )
 
@@ -121,7 +132,7 @@ def tile_picked_sminhinge_none_p_kernel(
             return dst, src
 
         def w2_quantize(grouped, t):
-            codes = keep.tile([P, P], U32, name="w2_codes%d" % t, tag="w2_slot%d" % t, align_bytes=64)
+            codes = keep.tile([P, P], U32, name="w2_codes%d" % t, tag=("w2_slot0", "w2_slot1", "z_slot2", "w2_slot0")[t], align_bytes=64)
             scales = keep.tile([P, P], U8, name="w2_scales%d" % t, align_bytes=64)
             nc.vector.quantize_mx(out=codes[:].bitcast(FP8X4), scales=scales[:], in_=grouped[:])
             return codes, scales
@@ -132,59 +143,59 @@ def tile_picked_sminhinge_none_p_kernel(
             first_product(y_half, 0, half)
             exponential(ex_window[0], y_half, cols(half, HALF))
             exponential(ex_plain[0], y_half, cols(half, HALF))
-        y_bank = {}
-        for t in (3, 1, 2):
-            y_bank[t] = bank(1 + t)
+        for t in range(1, PACK):
+            y_bank = bank(1 + t)
             for half in range(2):
-                first_product(y_bank[t], t, half)
-        exponential(ex_window[3], y_bank[3], whole)
-        nc.sync.dma_start(ex_plain[3][:], ex_window[3][:])
-        for half in range(2):
-            pair_sums(0, half)
+                first_product(y_bank, t, half)
+            exponential(ex_window[t], y_bank, whole)
+            exponential(ex_plain[t], y_bank, whole)
+        for t in range(2):
+            for half in range(2):
+                pair_sums(t, half)
         w2_first = keep.tile([P, PACK * P], BF16, name="w2_grouped0", align_bytes=64)
         nc.vector.tensor_copy(*w2_views(w2_first, 0))
-        for t in (1, 2):
-            exponential(ex_window[t], y_bank[t], whole)
-            exponential(ex_plain[t], y_bank[t], whole)
-        pair_sums(1, 0)
+        pair_sums(2, 0)
         w2_quantized = [w2_quantize(w2_first, 0)]
-        pair_sums(1, 1)
-        for half in range(2):
-            for t in (2, 3):
-                pair_sums(t, half)
+        pair_sums(3, 0)
+        pair_sums(2, 1)
+        pair_sums(3, 1)
 
         z_codes = keep.tile([P, S], U32, name="z_codes", align_bytes=64)
         z_scales = keep.tile([P, S], U8, name="z_scales", align_bytes=64)
+        pieces = [cols(quarter, QUARTER) for quarter in range(4)]
         z_rounded = []
-        for quarter in range(4):
-            logs = keep.tile([P, QUARTER, PACK], F32, name="logs%d" % quarter)
+
+        def quantize_z(index):
+            nc.vector.quantize_mx(
+                out=z_codes[:, pieces[index]].bitcast(FP8X4), scales=z_scales[:, pieces[index]], in_=z_rounded[index][:]
+            )
+
+        for index, piece in enumerate(pieces):
+            width = piece.stop - piece.start
+            logs = keep.tile([P, width, PACK], F32, name="logs%d" % index)
             nc.scalar.activation(
                 logs[:].rearrange("p (c i) t -> p c t i", i=4),
-                sums[quarter // 2][:, :, cols(quarter % 2, QUARTER)].rearrange("p t (c i) -> p c t i", i=4),
+                sums[index // 2][:, :, cols(index % 2, QUARTER)].rearrange("p t (c i) -> p c t i", i=4),
                 ACT.Ln,
             )
-            rounded = keep.tile([P, QUARTER * PACK], BF16, name="z_rounded%d" % quarter, tag="z_slot%d" % quarter, align_bytes=64)
+            rounded = keep.tile(
+                [P, width * PACK], BF16, name="z_rounded%d" % index, tag="z_slot%d" % index, align_bytes=64
+            )
             nc.vector.scalar_tensor_tensor(
                 rounded[:].rearrange("p (n t) -> p n t", t=PACK),
                 logs[:],
                 -1.0,
-                gain[:].unsqueeze(1).to_broadcast([P, QUARTER, PACK]),
+                gain[:].unsqueeze(1).to_broadcast([P, width, PACK]),
                 ALU.mult,
                 ALU.mult,
             )
             z_rounded.append(rounded)
-            if quarter > 0:
-                nc.vector.quantize_mx(
-                    out=z_codes[:, cols(quarter - 1, QUARTER)].bitcast(FP8X4),
-                    scales=z_scales[:, cols(quarter - 1, QUARTER)],
-                    in_=z_rounded[quarter - 1][:],
-                )
-        nc.vector.quantize_mx(
-            out=z_codes[:, cols(3, QUARTER)].bitcast(FP8X4), scales=z_scales[:, cols(3, QUARTER)], in_=z_rounded[3][:]
-        )
+            if index > 0:
+                quantize_z(index - 1)
+        quantize_z(len(pieces) - 1)
 
-        h_window = [keep.tile([P, S], F32, name="h_window%d" % t) for t in range(PACK)]
-        h_less = [keep.tile([P, S], F32, name="h_less%d" % t) for t in range(PACK)]
+        h_window = wide
+        h_less = {t: keep.tile([P, S], F32, name="h_less%d" % t) for t in range(TURNED, PACK)}
 
         def second_product(target, t, columns):
             nc.tensor.matmul_mx(
@@ -198,23 +209,27 @@ def tile_picked_sminhinge_none_p_kernel(
             )
 
         def leave_bank(source, t, columns):
-            nc.scalar.activation(h_window[t][:, columns], source[:, columns], ACT.Copy)
-            nc.scalar.activation(h_less[t][:, columns], source[:, columns], ACT.Copy, bias=-0.5)
+            if t < TURNED:
+                nc.scalar.activation(h_window[t][:, columns], source[:, columns], ACT.Copy, scale=-1.0)
+            else:
+                nc.scalar.activation(h_window[t][:, columns], source[:, columns], ACT.Copy)
+                nc.scalar.activation(h_less[t][:, columns], source[:, columns], ACT.Copy, bias=-0.5)
 
-        early, late = bank(5), bank(6)
-        for quarter in range(3):
-            second_product(early, 0, cols(quarter, QUARTER))
-        leave_bank(early, 0, slice(0, 3 * QUARTER))
-        second_product(late, 0, cols(3, QUARTER))
-        leave_bank(late, 0, cols(3, QUARTER))
+        early = bank(5)
+        for piece in pieces[:2]:
+            second_product(early, 0, piece)
+        leave_bank(early, 0, cols(0, HALF))
+        late = [bank(6), bank(7)]
+        for index in range(2):
+            second_product(late[index], 0, pieces[2 + index])
+            leave_bank(late[index], 0, pieces[2 + index])
         for t in range(1, PACK):
+            grouped = keep.tile(
+                [P, PACK * P], BF16, name="w2_grouped%d" % t, tag="z_slot%d" % ((t - 2) % 4), align_bytes=64
+            )
             if t == 1:
-                grouped = keep.tile([P, PACK * P], BF16, name="w2_grouped1", tag="z_slot3", align_bytes=64)
                 nc.vector.tensor_copy(*w2_views(grouped, t))
             else:
-                grouped = keep.tile(
-                    [P, PACK * P], BF16, name="w2_grouped%d" % t, tag="w2_slot%d" % (t - 2), align_bytes=64
-                )
                 nc.scalar.copy(*w2_views(grouped, t))
             w2_quantized.append(w2_quantize(grouped, t))
             h_bank = bank(t - 1)
@@ -222,27 +237,61 @@ def tile_picked_sminhinge_none_p_kernel(
             leave_bank(h_bank, t, whole)
 
         out_rows = out.rearrange("(b t s) n -> t b s n", b=16, t=PACK)
-        steps = [(t, half) for t in range(PACK) for half in range(2)]
-        margins = {}
+        terms = []
+        for t in range(TURNED):
+            first = keep.tile([P, S], F32, name="first%d" % t)
+            nc.vector.tensor_scalar(first[:], h_window[t][:].indirect(n2_sb[:]), -1.0, 0.5, ALU.mult, ALU.add)
+            gap = keep.tile([P, S], F32, name="gap%d" % t, tag="turn_slot%d" % t)
+            nc.vector.tensor_tensor(gap[:], h_window[t][:].indirect(n3_sb[:]), first[:], ALU.add)
+            excess = keep.tile([P, S], F32, name="excess%d" % t)
+            nc.scalar.activation(excess[:], gap[:], ACT.Relu, bias=one_half[:], scale=-1.0)
+            terms.append((first, h_window[t], excess))
+        turned = []
+        for t in range(TURNED):
+            total = bank(3 + 2 * t)
+            for block in range(4):
+                for index, term in enumerate(terms[t]):
+                    nc.tensor.matmul(
+                        total[:, cols(block, P)],
+                        term[:, cols(block, P)],
+                        identity[:],
+                        is_transpose=True,
+                        start=index == 0,
+                        stop=index == len(terms[t]) - 1,
+                    )
+            turned.append(keep.tile([P, S], F32, name="turned%d" % t, tag="turn_slot%d" % (TURNED - 1 - t)))
+            nc.scalar.activation(turned[t][:], total[:], ACT.Relu)
+        for t in range(TURNED):
+            back = bank(4 + 2 * t)
+            for block in range(4):
+                nc.tensor.transpose(back[:, cols(block, P)], turned[t][:, cols(block, P)], identity[:])
+            result = keep.tile([P, S], F32, name="turned_result%d" % t)
+            nc.scalar.activation(result[:], back[:], ACT.Copy)
+            nc.scalar.dma_start(out_rows[t], result[:])
 
-        def finish(t, half):
-            result = keep.tile([P, HALF], F32, name="result%d_%d" % (t, half))
-            a, b = margins[t, half]
+        halves = [cols(half, HALF) for half in range(2)]
+        steps = [(t, columns) for t in range(TURNED, PACK) for columns in (halves if t == PACK - 1 else [whole])]
+        margins = []
+
+        def finish(index):
+            t, columns = steps[index]
+            result = keep.tile([P, columns.stop - columns.start], F32, name="result%d" % index)
+            a, b = margins[index]
             nc.vector.scalar_tensor_tensor(result[:], a[:], 0.0, b[:], ALU.max, ALU.max)
-            nc.sync.dma_start(out_rows[t][:, :, cols(half, HALF)], result[:])
+            nc.sync.dma_start(out_rows[t][:, :, columns], result[:])
 
-        for index, (t, half) in enumerate(steps):
+        for index, (t, columns) in enumerate(steps):
             pair = []
             for name, places in (("a", n2_sb), ("b", n3_sb)):
-                margin = keep.tile([P, HALF], F32, name="margin_%s%d_%d" % (name, t, half))
+                margin = keep.tile([P, columns.stop - columns.start], F32, name="margin_%s%d" % (name, index))
                 nc.vector.tensor_tensor(
                     margin[:],
-                    h_window[t][:].indirect(places[:, cols(half, LIST_COLS // 2)]),
-                    h_less[t][:, cols(half, HALF)],
+                    h_window[t][:].indirect(entries(places, columns)),
+                    h_less[t][:, columns],
                     ALU.subtract,
                 )
                 pair.append(margin)
                 if name == "a" and index > 0:
-                    finish(*steps[index - 1])
-            margins[t, half] = pair
-        finish(*steps[-1])
+                    finish(index - 1)
+            margins.append(pair)
+        finish(len(steps) - 1)

@@ -40,14 +40,12 @@ def tile_picked_sminhinge_none_p_kernel(
             nc.sync.dma_start(tile[:], source)
             return tile
 
-        def load_weight_half(name, w, half):
-            raw = keep.tile([P, PACK, HALF], F32, name="%s_raw%d" % (name, half))
-            nc.sync.dma_start(raw[:], w.rearrange("(p j) c -> p j c", j=PACK)[:, :, cols(half, HALF)])
-            return raw
+        def load_w1_rows(pair):
+            nc.sync.dma_start(w1_raw[:, cols(pair, 2), :], w1.rearrange("(p j) c -> p j c", j=PACK)[:, cols(pair, 2), :])
 
-        def deal_views(grouped, raw, half):
-            dst = grouped[:].rearrange("p (t m j) -> p m j t", t=PACK, j=PACK)[:, cols(half, P // 2), :, :]
-            src = raw[:].rearrange("p j (m t) -> p m j t", t=PACK)
+        def deal_views(pair):
+            dst = w1_grouped[pair][:].rearrange("p (t m j) -> p m j t", t=2, j=PACK)
+            src = w1_raw[:].rearrange("p j (m t) -> p m j t", t=PACK)[:, :, :, cols(pair, 2)]
             return dst, src
 
         def bank(index):
@@ -56,10 +54,11 @@ def tile_picked_sminhinge_none_p_kernel(
         x_scale_table = keep.tile([P, T], U8, name="x_scale_table")
         nc.vector.memset(x_scale_table[:].bitcast(I32), 0)
         offs_sb = load_list("offs_sb", offs)
-        w1_raw = [load_weight_half("w1", w1, 0)]
+        w1_raw = keep.tile([P, PACK, H], F32, name="w1_raw")
+        load_w1_rows(0)
         for r in range(4):
             nc.sync.dma_start(x_scale_table[r:P:32, :].bitcast(I32), x_scales[0, r:16:4, :].bitcast(I32))
-        w1_raw.append(load_weight_half("w1", w1, 1))
+        load_w1_rows(1)
         x_word_table = keep.tile([P, T], I32, name="x_word_table")
         nc.sync.dma_start(x_word_table[:], x_words[0].rearrange("p n t -> p (n t)").bitcast(I32))
         n1_sb = load_list("n1_sb", n1)
@@ -75,16 +74,22 @@ def tile_picked_sminhinge_none_p_kernel(
         one_half = keep.tile([P, 1], F32, name="one_half")
         nc.gpsimd.memset(one_half[:], 0.5)
 
-        w1_grouped = keep.tile([P, PACK * H], BF16, name="w1_grouped", align_bytes=64)
-        dst, src = deal_views(w1_grouped, w1_raw[0], 0)
-        nc.scalar.activation(dst, src, ACT.Copy)
-        dst, src = deal_views(w1_grouped, w1_raw[1], 1)
-        nc.vector.tensor_copy(dst, src)
+        w1_grouped = [
+            keep.tile([P, 2 * PACK * P], BF16, name="w1_grouped%d" % pair, align_bytes=64) for pair in range(2)
+        ]
         x_scale_picked = keep.tile([P, S], U8, name="x_scale_picked", align_bytes=64)
         nc.vector.tensor_copy(x_scale_picked[:], x_scale_table[:].indirect(offs_sb[:]))
+        nc.vector.tensor_copy(*deal_views(0))
+        dst, src = deal_views(1)
+        for pair in range(2):
+            nc.scalar.activation(dst[:, :, cols(pair, 2), :], src[:, :, cols(pair, 2), :], ACT.Copy)
         w1_codes = keep.tile([P, H], U32, name="w1_codes", align_bytes=64)
         w1_scales = keep.tile([P, H], U8, name="w1_scales", align_bytes=64)
-        nc.vector.quantize_mx(out=w1_codes[:].bitcast(FP8X4), scales=w1_scales[:], in_=w1_grouped[:])
+        for pair in range(2):
+            columns = cols(pair, 2 * P)
+            nc.vector.quantize_mx(
+                out=w1_codes[:, columns].bitcast(FP8X4), scales=w1_scales[:, columns], in_=w1_grouped[pair][:]
+            )
 
         x_picked = []
         for half in range(2):
@@ -132,26 +137,31 @@ def tile_picked_sminhinge_none_p_kernel(
             return dst, src
 
         def w2_quantize(grouped, t):
-            codes = keep.tile([P, P], U32, name="w2_codes%d" % t, tag=("w2_slot0", "w2_slot1", "z_slot2", "w2_slot0")[t], align_bytes=64)
+            codes = keep.tile([P, P], U32, name="w2_codes%d" % t, tag=("w2_slot0", "w2_slot1", "z_slot2", "w2_slot3")[t], align_bytes=64)
             scales = keep.tile([P, P], U8, name="w2_scales%d" % t, align_bytes=64)
             nc.vector.quantize_mx(out=codes[:].bitcast(FP8X4), scales=scales[:], in_=grouped[:])
             return codes, scales
 
         whole = slice(0, S)
         for half in range(2):
-            y_half = bank(half)
-            first_product(y_half, 0, half)
-            exponential(ex_window[0], y_half, cols(half, HALF))
-            exponential(ex_plain[0], y_half, cols(half, HALF))
-        for t in range(1, PACK):
-            y_bank = bank(1 + t)
+            columns = cols(half, HALF)
+            y_halves = [bank(2 * t + half) for t in range(2)]
+            for t in range(2):
+                first_product(y_halves[t], t, half)
+                exponential(ex_window[t], y_halves[t], columns)
+            nc.vector.tensor_copy(ex_plain[0][:, columns], ex_window[0][:, columns])
+            exponential(ex_plain[1], y_halves[1], columns)
+        for t in range(2, PACK):
+            y_bank = bank(2 + t)
             for half in range(2):
                 first_product(y_bank, t, half)
             exponential(ex_window[t], y_bank, whole)
-            exponential(ex_plain[t], y_bank, whole)
-        for t in range(2):
-            for half in range(2):
-                pair_sums(t, half)
+        exponential(ex_plain[3], y_bank, whole)
+        for half in range(2):
+            pair_sums(0, half)
+        pair_sums(1, 0)
+        nc.vector.tensor_copy(ex_plain[2], ex_window[2][:, whole])
+        pair_sums(1, 1)
         w2_first = keep.tile([P, PACK * P], BF16, name="w2_grouped0", align_bytes=64)
         nc.vector.tensor_copy(*w2_views(w2_first, 0))
         pair_sums(2, 0)
@@ -215,7 +225,7 @@ def tile_picked_sminhinge_none_p_kernel(
                 nc.scalar.activation(h_window[t][:, columns], source[:, columns], ACT.Copy)
                 nc.scalar.activation(h_less[t][:, columns], source[:, columns], ACT.Copy, bias=-0.5)
 
-        early = bank(5)
+        early = bank(0)
         for piece in pieces[:2]:
             second_product(early, 0, piece)
         leave_bank(early, 0, cols(0, HALF))
@@ -225,14 +235,14 @@ def tile_picked_sminhinge_none_p_kernel(
             leave_bank(late[index], 0, pieces[2 + index])
         for t in range(1, PACK):
             grouped = keep.tile(
-                [P, PACK * P], BF16, name="w2_grouped%d" % t, tag="z_slot%d" % ((t - 2) % 4), align_bytes=64
+                [P, PACK * P], BF16, name="w2_grouped%d" % t, tag=("z_slot3", "z_slot0", "w2_slot0")[t - 1], align_bytes=64
             )
             if t == 1:
                 nc.vector.tensor_copy(*w2_views(grouped, t))
             else:
                 nc.scalar.copy(*w2_views(grouped, t))
             w2_quantized.append(w2_quantize(grouped, t))
-            h_bank = bank(t - 1)
+            h_bank = bank(t)
             second_product(h_bank, t, whole)
             leave_bank(h_bank, t, whole)
 
@@ -248,7 +258,7 @@ def tile_picked_sminhinge_none_p_kernel(
             terms.append((first, h_window[t], excess))
         turned = []
         for t in range(TURNED):
-            total = bank(3 + 2 * t)
+            total = bank(4 + 2 * t)
             for block in range(4):
                 for index, term in enumerate(terms[t]):
                     nc.tensor.matmul(
@@ -262,7 +272,7 @@ def tile_picked_sminhinge_none_p_kernel(
             turned.append(keep.tile([P, S], F32, name="turned%d" % t, tag="turn_slot%d" % (TURNED - 1 - t)))
             nc.scalar.activation(turned[t][:], total[:], ACT.Relu)
         for t in range(TURNED):
-            back = bank(4 + 2 * t)
+            back = bank(5 + 2 * t)
             for block in range(4):
                 nc.tensor.transpose(back[:, cols(block, P)], turned[t][:, cols(block, P)], identity[:])
             result = keep.tile([P, S], F32, name="turned_result%d" % t)

from contextlib import ExitStack

import concourse.mybir as mybir
from concourse.masks import make_identity

K, T, S, H, N = 512, 2048, 512, 512, 512
FLOPS = 2 * K * H * S + 2 * H * N * S

F32 = mybir.dt.float32
BF16 = mybir.dt.bfloat16
I32 = mybir.dt.int32
U32 = mybir.dt.uint32
U16 = mybir.dt.uint16
U8 = mybir.dt.uint8
FP8X4 = mybir.dt.float8_e4m3fn_x4
ACT = mybir.ActivationFunctionType
ALU = mybir.AluOpType

P = 128
PACK = 4
HALF = S // 2
QUARTER = S // 4
LIST_COLS = S // 16
TURNED = 1


def tile_picked_sminhinge_none_p_kernel(
    tc, x_words, x_scales, w1, gn, w2, offs, n1, n2, n3, out
):
    nc = tc.nc
    with ExitStack() as ctx:
        keep = ctx.enter_context(tc.tile_pool(name="keep", bufs=1))
        psum = ctx.enter_context(tc.psum_pool(name="psum", bufs=1))

        def cols(part, width):
            return slice(part * width, (part + 1) * width)

        def load_list(name, source):
            tile = keep.tile([P, LIST_COLS], U16, name=name)
            nc.sync.dma_start(tile[:], source)
            return tile

        def load_w1_rows(pair):
            nc.sync.dma_start(w1_raw[:, cols(pair, 2), :], w1.rearrange("(p j) c -> p j c", j=PACK)[:, cols(pair, 2), :])

        def deal_views(pair):
            dst = w1_grouped[pair][:].rearrange("p (t m j) -> p m j t", t=2, j=PACK)
            src = w1_raw[:].rearrange("p j (m t) -> p m j t", t=PACK)[:, :, :, cols(pair, 2)]
            return dst, src

        def bank(index):
            return psum.tile([P, S], F32, name="bank%d" % index, tag="bank%d" % index)

        x_scale_table = keep.tile([P, T], U8, name="x_scale_table")
        nc.vector.memset(x_scale_table[:].bitcast(I32), 0)
        offs_sb = load_list("offs_sb", offs)
        w1_raw = keep.tile([P, PACK, H], F32, name="w1_raw")
        load_w1_rows(0)
        for r in range(4):
            nc.sync.dma_start(x_scale_table[r:P:32, :].bitcast(I32), x_scales[0, r:16:4, :].bitcast(I32))
        load_w1_rows(1)
        x_word_table = keep.tile([P, T], I32, name="x_word_table")
        nc.sync.dma_start(x_word_table[:], x_words[0].rearrange("p n t -> p (n t)").bitcast(I32))
        n1_sb = load_list("n1_sb", n1)
        w2_raw = keep.tile([P, PACK, N], F32, name="w2_raw")
        nc.sync.dma_start(w2_raw[:], w2.rearrange("(p j) c -> p j c", j=PACK))
        gain = keep.tile([P, PACK], F32, name="gain")
        nc.sync.dma_start(gain[:], gn.rearrange("(p t) one -> p (t one)", t=PACK))
        n2_sb = load_list("n2_sb", n2)
        n3_sb = load_list("n3_sb", n3)

        identity = keep.tile([P, P], F32, name="identity")
        make_identity(nc, identity[:])
        one_half = keep.tile([P, 1], F32, name="one_half")
        nc.gpsimd.memset(one_half[:], 0.5)

        w1_grouped = [
            keep.tile([P, 2 * PACK * P], BF16, name="w1_grouped%d" % pair, align_bytes=64) for pair in range(2)
        ]
        x_scale_picked = keep.tile([P, S], U8, name="x_scale_picked", align_bytes=64)
        nc.vector.tensor_copy(x_scale_picked[:], x_scale_table[:].indirect(offs_sb[:]))
        nc.vector.tensor_copy(*deal_views(0))
        dst, src = deal_views(1)
        for pair in range(2):
            nc.scalar.activation(dst[:, :, cols(pair, 2), :], src[:, :, cols(pair, 2), :], ACT.Copy)
        w1_codes = keep.tile([P, H], U32, name="w1_codes", align_bytes=64)
        w1_scales = keep.tile([P, H], U8, name="w1_scales", align_bytes=64)
        for pair in range(2):
            columns = cols(pair, 2 * P)
            nc.vector.quantize_mx(
                out=w1_codes[:, columns].bitcast(FP8X4), scales=w1_scales[:, columns], in_=w1_grouped[pair][:]
            )

        x_picked = []
        for half in range(2):
            words = keep.tile([P, HALF], U32, name="x_picked%d" % half, align_bytes=64)
            nc.vector.tensor_copy(
                words[:], x_word_table[:].bitcast(U32).indirect(offs_sb[:, cols(half, LIST_COLS // 2)])
            )
            x_picked.append(words)

        first_window = keep.tile([P, S], F32, name="first_window")
        wide = [keep.tile([P, 2 * S], F32, name="wide%d" % t) for t in range(PACK)]
        ex_window = [first_window, wide[1], wide[2], wide[3]]
        ex_plain = [wide[t ^ 1][:, S : 2 * S] for t in range(PACK)]
        sums = [keep.tile([P, PACK, HALF], F32, name="sums%d" % half) for half in range(2)]

        def first_product(target, t, half):
            nc.tensor.matmul_mx(
                out=target[:, cols(half, HALF)],
                lhsT=w1_codes[:, cols(t, P)].bitcast(FP8X4),
                lhsT_scale=w1_scales[:, cols(t, P)],
                rhs=x_picked[half][:].bitcast(FP8X4),
                rhs_scale=x_scale_picked[:, cols(half, HALF)],
                start=True,
                stop=True,
            )

        def exponential(target, source, columns):
            nc.scalar.activation(target[:, columns], source[:, columns], ACT.Exp, scale=-1.0)

        def entries(places, columns):
            return places[:, columns.start // 16 : columns.stop // 16]

        def pair_sums(t, half):
            columns = cols(half, HALF)
            nc.vector.tensor_tensor(
                sums[half][:, t, :],
                ex_window[t][:].indirect(entries(n1_sb, columns)),
                ex_plain[t][:, columns],
                ALU.add,
            )

        def w2_views(grouped, t):
            dst = grouped[:].rearrange("p (b c i j) -> p b c j i", b=16, c=2, i=4)
            src = w2_raw[:].rearrange("p j (b t c i) -> p t b c j i", b=16, t=PACK, c=2)[:, t]
            return dst, src

        def w2_quantize(grouped, t):
            codes = keep.tile([P, P], U32, name="w2_codes%d" % t, tag=("w2_slot0", "w2_slot1", "z_slot2", "w2_slot3")[t], align_bytes=64)
            scales = keep.tile([P, P], U8, name="w2_scales%d" % t, align_bytes=64)
            nc.vector.quantize_mx(out=codes[:].bitcast(FP8X4), scales=scales[:], in_=grouped[:])
            return codes, scales

        whole = slice(0, S)
        for half in range(2):
            columns = cols(half, HALF)
            y_halves = [bank(2 * t + half) for t in range(2)]
            for t in range(2):
                first_product(y_halves[t], t, half)
                exponential(ex_window[t], y_halves[t], columns)
            nc.vector.tensor_copy(ex_plain[0][:, columns], ex_window[0][:, columns])
            exponential(ex_plain[1], y_halves[1], columns)
        for t in range(2, PACK):
            y_bank = bank(2 + t)
            for half in range(2):
                first_product(y_bank, t, half)
            exponential(ex_window[t], y_bank, whole)
        exponential(ex_plain[3], y_bank, whole)
        for half in range(2):
            pair_sums(0, half)
        pair_sums(1, 0)
        nc.vector.tensor_copy(ex_plain[2], ex_window[2][:, whole])
        pair_sums(1, 1)
        w2_first = keep.tile([P, PACK * P], BF16, name="w2_grouped0", align_bytes=64)
        nc.vector.tensor_copy(*w2_views(w2_first, 0))
        pair_sums(2, 0)
        w2_quantized = [w2_quantize(w2_first, 0)]
        pair_sums(3, 0)
        pair_sums(2, 1)
        pair_sums(3, 1)

        z_codes = keep.tile([P, S], U32, name="z_codes", align_bytes=64)
        z_scales = keep.tile([P, S], U8, name="z_scales", align_bytes=64)
        pieces = [cols(quarter, QUARTER) for quarter in range(4)]
        z_rounded = []

        def quantize_z(index):
            nc.vector.quantize_mx(
                out=z_codes[:, pieces[index]].bitcast(FP8X4), scales=z_scales[:, pieces[index]], in_=z_rounded[index][:]
            )

        for index, piece in enumerate(pieces):
            width = piece.stop - piece.start
            logs = keep.tile([P, width, PACK], F32, name="logs%d" % index)
            nc.scalar.activation(
                logs[:].rearrange("p (c i) t -> p c t i", i=4),
                sums[index // 2][:, :, cols(index % 2, QUARTER)].rearrange("p t (c i) -> p c t i", i=4),
                ACT.Ln,
            )
            rounded = keep.tile(
                [P, width * PACK], BF16, name="z_rounded%d" % index, tag="z_slot%d" % index, align_bytes=64
            )
            nc.vector.scalar_tensor_tensor(
                rounded[:].rearrange("p (n t) -> p n t", t=PACK),
                logs[:],
                -1.0,
                gain[:].unsqueeze(1).to_broadcast([P, width, PACK]),
                ALU.mult,
                ALU.mult,
            )
            z_rounded.append(rounded)
            if index > 0:
                quantize_z(index - 1)
        quantize_z(len(pieces) - 1)

        h_window = wide
        h_less = {t: keep.tile([P, S], F32, name="h_less%d" % t) for t in range(TURNED, PACK)}

        def second_product(target, t, columns):
            nc.tensor.matmul_mx(
                out=target[:, columns],
                lhsT=w2_quantized[t][0][:].bitcast(FP8X4),
                lhsT_scale=w2_quantized[t][1][:],
                rhs=z_codes[:, columns].bitcast(FP8X4),
                rhs_scale=z_scales[:, columns],
                start=True,
                stop=True,
            )

        def leave_bank(source, t, columns):
            if t < TURNED:
                nc.scalar.activation(h_window[t][:, columns], source[:, columns], ACT.Copy, scale=-1.0)
            else:
                nc.scalar.activation(h_window[t][:, columns], source[:, columns], ACT.Copy)
                nc.scalar.activation(h_less[t][:, columns], source[:, columns], ACT.Copy, bias=-0.5)

        early = bank(0)
        for piece in pieces[:2]:
            second_product(early, 0, piece)
        leave_bank(early, 0, cols(0, HALF))
        late = [bank(6), bank(7)]
        for index in range(2):
            second_product(late[index], 0, pieces[2 + index])
            leave_bank(late[index], 0, pieces[2 + index])
        for t in range(1, PACK):
            grouped = keep.tile(
                [P, PACK * P], BF16, name="w2_grouped%d" % t, tag=("z_slot3", "z_slot0", "w2_slot0")[t - 1], align_bytes=64
            )
            if t == 1:
                nc.vector.tensor_copy(*w2_views(grouped, t))
            else:
                nc.scalar.copy(*w2_views(grouped, t))
            w2_quantized.append(w2_quantize(grouped, t))
            h_bank = bank(t)
            second_product(h_bank, t, whole)
            leave_bank(h_bank, t, whole)

        out_rows = out.rearrange("(b t s) n -> t b s n", b=16, t=PACK)
        terms = []
        for t in range(TURNED):
            first = keep.tile([P, S], F32, name="first%d" % t)
            nc.vector.tensor_scalar(first[:], h_window[t][:].indirect(n2_sb[:]), -1.0, 0.5, ALU.mult, ALU.add)
            gap = keep.tile([P, S], F32, name="gap%d" % t, tag="turn_slot%d" % t)
            nc.vector.tensor_tensor(gap[:], h_window[t][:].indirect(n3_sb[:]), first[:], ALU.add)
            excess = keep.tile([P, S], F32, name="excess%d" % t)
            nc.scalar.activation(excess[:], gap[:], ACT.Relu, bias=one_half[:], scale=-1.0)
            terms.append((first, h_window[t], excess))
        turned = []
        for t in range(TURNED):
            total = bank(4 + 2 * t)
            for block in range(4):
                for index, term in enumerate(terms[t]):
                    nc.tensor.matmul(
                        total[:, cols(block, P)],
                        term[:, cols(block, P)],
                        identity[:],
                        is_transpose=True,
                        start=index == 0,
                        stop=index == len(terms[t]) - 1,
                    )
            turned.append(keep.tile([P, S], F32, name="turned%d" % t, tag="turn_slot%d" % (TURNED - 1 - t)))
            nc.scalar.activation(turned[t][:], total[:], ACT.Relu)
        for t in range(TURNED):
            back = bank(5 + 2 * t)
            for block in range(4):
                nc.tensor.transpose(back[:, cols(block, P)], turned[t][:, cols(block, P)], identity[:])
            result = keep.tile([P, S], F32, name="turned_result%d" % t)
            nc.scalar.activation(result[:], back[:], ACT.Copy)
            nc.scalar.dma_start(out_rows[t], result[:])

        halves = [cols(half, HALF) for half in range(2)]
        steps = [(t, columns) for t in range(TURNED, PACK) for columns in (halves if t == PACK - 1 else [whole])]
        margins = []

        def finish(index):
            t, columns = steps[index]
            result = keep.tile([P, columns.stop - columns.start], F32, name="result%d" % index)
            a, b = margins[index]
            nc.vector.scalar_tensor_tensor(result[:], a[:], 0.0, b[:], ALU.max, ALU.max)
            nc.sync.dma_start(out_rows[t][:, :, columns], result[:])

        for index, (t, columns) in enumerate(steps):
            pair = []
            for name, places in (("a", n2_sb), ("b", n3_sb)):
                margin = keep.tile([P, columns.stop - columns.start], F32, name="margin_%s%d" % (name, index))
                nc.vector.tensor_tensor(
                    margin[:],
                    h_window[t][:].indirect(entries(places, columns)),
                    h_less[t][:, columns],
                    ALU.subtract,
                )
                pair.append(margin)
                if name == "a" and index > 0:
                    finish(index - 1)
            margins.append(pair)
        finish(len(steps) - 1)
